import numpy as np
import ml_dtypes


def mxq(x, axis, fmt="e4m3"):
    dtype, down = {"e4m3": (ml_dtypes.float8_e4m3fn, 7), "e5m2": (ml_dtypes.float8_e5m2, 14)}[fmt]
    v = np.moveaxis(np.asarray(x, np.float32).astype(ml_dtypes.bfloat16).astype(np.float64), axis, -1)
    blocks = v.reshape(v.shape[:-1] + (-1, 32))
    amax = np.abs(blocks).max(-1, keepdims=True)
    byte = np.maximum(np.where(amax > 0, np.frexp(amax)[1] - 1 + 127, 0) - down, 1)
    scale = np.exp2(byte - 127.0)
    codes = (blocks / scale).astype(np.float32).astype(dtype).astype(np.float64)
    return np.moveaxis((codes * scale).reshape(v.shape), -1, axis)


WIDE = False


def mx_kscale(k):
    if not WIDE:
        return np.ones(k)
    levels = np.array([10, -10, 5, -5, 0])
    if k % 512:
        return np.exp2(np.random.permutation(np.resize(levels, k // 32))).repeat(32)
    a = np.empty((k // 512, 16))
    for p in range(k // 512):
        a[p, :8] = np.random.permutation(np.resize(levels, 8))
        for g in range(8):
            far = levels[np.abs(levels - a[p, g]) >= 10]
            a[p, g + 8] = far[np.random.randint(len(far))]
    return np.exp2(a.ravel()).repeat(32)


def f64(x):
    return np.asarray(x).astype(np.float64)


def striped(idx):
    return np.tile(idx.reshape(-1, 16).T, (8, 1)).astype(np.uint16)


def unstriped(offs):
    return offs[:16].T.reshape(-1).astype(np.int64)


def striped8(idx):
    return np.concatenate([x.reshape(-1, 16).T for x in idx]).astype(np.uint16)


def runs(offs, k):
    lists = np.stack([offs[16 * r : 16 * r + 16].T.reshape(-1) for r in range(8)]).astype(np.int64)
    return lists[np.arange(k) % 512 // 64]


def pack_weight(w):
    k, n = w.shape
    w = f64(np.asarray(w, np.float32).astype(ml_dtypes.bfloat16)).reshape(k // 32, 32, n)
    amax = np.abs(w).max(1)
    byte = np.clip(np.where(amax > 0, np.frexp(amax)[1] - 1 + 127 - 7, 1), 1, 254)
    scaled = (w * np.exp2(127.0 - byte)[:, None, :]).reshape(k, n).astype(np.float32)
    words = np.ascontiguousarray(scaled.reshape(k // 512, 128, 4, n).transpose(0, 1, 3, 2)).astype(ml_dtypes.float8_e4m3fn).view(np.uint8)
    return words, np.ascontiguousarray(byte.astype(np.uint8).reshape(k // 512, 16, n))


def unpack_weight(words, scales):
    g, p, n, _ = words.shape
    vals = np.ascontiguousarray(words).view(ml_dtypes.float8_e4m3fn).astype(np.float64) * np.repeat(np.exp2(scales.astype(np.float64) - 127.0), 8, axis=1)[..., None]
    return vals.transpose(0, 1, 3, 2).reshape(g * 512, n)


def sigmoid(v):
    return 1.0 / (1.0 + np.exp(-np.maximum(v, -700.0)))


K, T, S, N, H, W = 512, 2048, 512, 512, 512, 256


def setup_inputs():
    n = np.random.standard_normal
    s = mx_kscale(K)[:, None]
    u = mx_kscale(H)
    packed_xT = pack_weight(n((K, T)) * s)
    perm = np.stack([np.random.permutation(S) for _ in range(8)])
    return {
        "x_words": packed_xT[0],
        "x_scales": packed_xT[1],
        "w1": (n((K, H)) / np.sqrt(K) / s).astype(np.float32),
        "gn": (np.random.uniform(0.5, 1.5, (H, 1)) * u[:, None]).astype(np.float32),
        "gm": (np.random.uniform(0.5, 1.5, (H, 1)) * u[:, None]).astype(np.float32),
        "w2": (n((H, N)) / np.sqrt(2 * H) / u[:, None]).astype(np.float32),
        "w3": (n((H, N)) / np.sqrt(2 * H) / u[:, None]).astype(np.float32),
        "offs": striped(np.random.permutation(T)[:S]),
        "n1": striped8(perm[:, :W]),
        "n2": striped8(perm[:, W:]),
        "n3": striped8(np.stack([np.random.permutation(S) for _ in range(8)])),
        "n4": striped8(np.stack([np.random.permutation(S) for _ in range(8)])),
        "n5": striped8(np.stack([np.random.permutation(S) for _ in range(8)])),
        "n6": striped8(np.stack([np.random.permutation(S) for _ in range(8)])),
    }


def reference(x_words, x_scales, w1, gn, gm, w2, w3, offs, n1, n2, n3, n4, n5, n6):
    xq = unpack_weight(x_words, x_scales)[:, unstriped(offs)]
    y = mxq(f64(w1), 0, "e4m3").T @ xq
    pa = y[np.arange(H)[:, None], runs(n1, H)]
    pb = y[np.arange(H)[:, None], runs(n2, H)]
    rb = np.maximum(0.5 * pa, pb)
    ra = pb - pa
    ds = np.zeros((H, S))
    ds[np.arange(H)[:, None], runs(n1, H)] = ra
    dt = ds.copy()
    dt[np.arange(H)[:, None], runs(n2, H)] = rb
    z = f64(gn) * dt
    st = y * (sigmoid(y[np.arange(H)[:, None], runs(n3, H)]))
    z2 = f64(gm) * (st - (st[np.arange(H)[:, None], runs(n4, H)]))
    h = mxq(f64(w2), 0, "e4m3").T @ mxq(z, 0, "e4m3") + mxq(f64(w3), 0, "e4m3").T @ mxq(z2, 0, "e4m3")
    pa2 = h[np.arange(N)[:, None], runs(n5, N)]
    kr = np.exp(-0.5 * ((h - pa2) ** 2))
    pb2 = h[np.arange(N)[:, None], runs(n6, N)]
    kr2 = np.exp(-0.5 * ((h - pb2) ** 2))
    return (kr * pa2 + kr2 * pb2) / (kr + kr2 + 0.5)

@@ -1,0 +1,290 @@
+from contextlib import ExitStack
+
+import concourse.mybir as mybir
+from concourse.masks import make_identity
+
+F32 = mybir.dt.float32
+BF16 = mybir.dt.bfloat16
+I32 = mybir.dt.int32
+U32 = mybir.dt.uint32
+U16 = mybir.dt.uint16
+U8 = mybir.dt.uint8
+FP8X4 = mybir.dt.float8_e4m3fn_x4
+ALU = mybir.AluOpType
+ACT = mybir.ActivationFunctionType
+
+P = 128
+PACK = 4
+T = 2048
+S = 512
+HALF = S // 2
+FLOPS = 3 * 2 * 512 * 512 * 512
+
+
+def tile_picked_joinlifthopgkern_none_p_kernel(
+    tc, x_words, x_scales, w1, gn, gm, w2, w3, offs, n1, n2, n3, n4, n5, n6, out
+):
+    nc = tc.nc
+    with ExitStack() as ctx:
+        lists = ctx.enter_context(tc.tile_pool(name="lists", bufs=1))
+        keep = ctx.enter_context(tc.tile_pool(name="keep", bufs=1))
+        psum = ctx.enter_context(tc.psum_pool(name="psum", bufs=1))
+
+        def load_list(src, name):
+            tile = lists.tile([P, src.shape[1]], U16, name=name)
+            nc.sync.dma_start(tile[:], src)
+            return tile
+
+        def half_of(list_tile, u):
+            cols = HALF // 16
+            return list_tile[:, u * cols : (u + 1) * cols]
+
+        def load_weight_half(w, u, name):
+            raw = keep.tile([P, PACK, HALF], F32, name=name)
+            nc.sync.dma_start(raw[:], w.rearrange("(p j) c -> p j c", j=PACK)[:, :, u * HALF : (u + 1) * HALF])
+            return raw
+
+        def deal_weight_half(copy, grouped, raw, u):
+            m_half = slice(u * P // 2, (u + 1) * P // 2)
+            copy(
+                grouped[:, :, m_half, :].rearrange("p t m j -> p m j t"),
+                raw[:].rearrange("p j (m t) -> p m j t", t=PACK),
+            )
+
+        def quantize(grouped, name, tag=""):
+            width = grouped.shape[1] // PACK
+            codes = keep.tile([P, width], U32, name=name + "_codes", align_bytes=64, tag=tag)
+            scales = keep.tile([P, width], U8, name=name + "_scales", align_bytes=64)
+            nc.vector.quantize_mx(out=codes[:].bitcast(FP8X4), scales=scales[:], in_=grouped)
+            return codes, scales
+
+        def interleave(copy, planes, name):
+            width = planes.shape[2]
+            grouped = keep.tile([P, width, PACK], BF16, name=name, align_bytes=64)
+            copy(
+                grouped[:].rearrange("p (c i) t -> p c t i", i=4),
+                planes.rearrange("p t (c i) -> p c t i", i=4),
+            )
+            return grouped[:].rearrange("p c t -> p (c t)")
+
+        def mx_pass(acc, weights, t, moving, cols, start, stop):
+            rows = slice(t * P, (t + 1) * P)
+            nc.tensor.matmul_mx(
+                out=acc,
+                lhsT=weights[0][:, rows].bitcast(FP8X4),
+                lhsT_scale=weights[1][:, rows],
+                rhs=moving[0][:, cols].bitcast(FP8X4),
+                rhs_scale=moving[1][:, cols],
+                start=start,
+                stop=stop,
+            )
+
+        halves = [slice(u * HALF, (u + 1) * HALF) for u in range(2)]
+
+        xs_all = keep.tile([P, T], U8, name="xs_all")
+        nc.gpsimd.memset(xs_all[:].bitcast(I32), 0)
+        for q in range(4):
+            nc.scalar.dma_start(
+                xs_all[32 * q : 32 * q + 4, :].bitcast(I32), x_scales[0, 4 * q : 4 * q + 4, :].bitcast(I32)
+            )
+        warm = keep.tile([P, 2], F32, name="warm")
+        nc.gpsimd.memset(warm[:, 0:1], 0.0)
+        nc.scalar.activation(warm[:, 1:2], warm[:, 0:1], ACT.Sigmoid)
+        offs_t = load_list(offs, "offs")
+        w1_raw = [load_weight_half(w1, u, "w1_raw%d" % u) for u in range(2)]
+        xw_all = keep.tile([P, T], I32, name="xw_all")
+        nc.sync.dma_start(xw_all[:], x_words[0].rearrange("p n t -> p (n t)").bitcast(I32))
+        n1_t, n2_t, n3_t = load_list(n1, "n1"), load_list(n2, "n2"), load_list(n3, "n3")
+        gn_t = keep.tile([P, PACK], F32, name="gn_t")
+        nc.sync.dma_start(gn_t[:], gn.rearrange("(p t) o -> p (t o)", t=PACK))
+        gm_t = keep.tile([P, PACK], F32, name="gm_t")
+        nc.sync.dma_start(gm_t[:], gm.rearrange("(p t) o -> p (t o)", t=PACK))
+        w2_raw = [load_weight_half(w2, u, "w2_raw%d" % u) for u in range(2)]
+        w3_raw = [load_weight_half(w3, u, "w3_raw%d" % u) for u in range(2)]
+        n4_t, n5_t, n6_t = load_list(n4, "n4"), load_list(n5, "n5"), load_list(n6, "n6")
+
+        ident = keep.tile([P, P], F32, name="ident")
+        make_identity(nc, ident[:])
+        gm_neg = keep.tile([P, PACK], F32, name="gm_neg")
+        nc.gpsimd.tensor_scalar(gm_neg[:], gm_t[:], -1.0, 0.0, ALU.mult, ALU.add)
+
+        xq_scales = keep.tile([P, S], U8, name="xq_scales", align_bytes=64)
+        nc.vector.tensor_copy(xq_scales[:], xs_all[:].indirect(offs_t[:]))
+        w1_bf = keep.tile([P, PACK, P, PACK], BF16, name="w1_bf", align_bytes=64)
+        deal_weight_half(nc.scalar.copy, w1_bf, w1_raw[0], 0)
+        deal_weight_half(nc.vector.tensor_copy, w1_bf, w1_raw[1], 1)
+        w1_q = quantize(w1_bf[:].rearrange("p t m j -> p (t m j)"), "w1")
+
+        xq_words = keep.tile([P, S], U32, name="xq_words", align_bytes=64)
+        for u in range(2):
+            nc.vector.tensor_copy(xq_words[:, halves[u]], xw_all[:].bitcast(U32).indirect(half_of(offs_t, u)))
+        xq = (xq_words, xq_scales)
+
+        y = []
+        for t in range(PACK):
+            acc = psum.tile([P, S], F32, name="y_acc%d" % t, tag="bank%d" % t)
+            if t == 0:
+                for u in range(2):
+                    mx_pass(acc[:, halves[u]], w1_q, t, xq, halves[u], True, True)
+            else:
+                mx_pass(acc[:], w1_q, t, xq, slice(0, S), True, True)
+            y_t = keep.tile([P, S], F32, name="y%d" % t)
+            nc.scalar.copy(y_t[:], acc[:])
+            y.append(y_t)
+
+        w2_bf = keep.tile([P, PACK, P, PACK], BF16, name="w2_bf", align_bytes=64)
+        w3_bf = keep.tile([P, PACK, P, PACK], BF16, name="w3_bf", align_bytes=64)
+        late_weights = [(w2_bf, w2_raw[0], 0), (w2_bf, w2_raw[1], 1), (w3_bf, w3_raw[0], 0), (w3_bf, w3_raw[1], 1)]
+        z_planes = keep.tile([P, PACK, S], BF16, name="z_planes")
+        h_window = [keep.tile([P, 2 * S], F32, name="h_window%d" % t) for t in range(PACK)]
+        h = [w[:, 0:S] for w in h_window]
+        sig = [w[:, S : 2 * S] for w in h_window]
+        pa_neg = [keep.tile([P, HALF], F32, name="pa_neg%d" % t) for t in range(PACK)]
+        pb = [keep.tile([P, HALF], F32, name="pb%d" % t) for t in range(PACK)]
+        st = [keep.tile([P, S], F32, name="st%d" % t) for t in range(PACK)]
+        st_copy = [keep.tile([P, S], F32, name="st_copy%d" % t) for t in range(PACK)]
+
+        def fetch_pa(t):
+            nc.vector.tensor_scalar(pa_neg[t][:], y[t][:].indirect(n1_t[:]), -1.0, 0.0, ALU.mult, ALU.add)
+
+        def fetch_pb(t):
+            nc.vector.tensor_copy(pb[t][:], y[t][:].indirect(n2_t[:]))
+
+        fetch_pa(0)
+        fetch_pb(0)
+        for t in range(PACK):
+            for u in range(2):
+                nc.scalar.activation(sig[t][:, halves[u]], y[t][:].indirect(half_of(n3_t, u)), ACT.Sigmoid)
+            rb = keep.tile([P, HALF], F32, name="rb%d" % t)
+            dt = keep.tile([P, S], F32, name="dt%d" % t)
+            if t + 1 < PACK:
+                fetch_pa(t + 1)
+            nc.vector.tensor_tensor(dt[:].indirect(n1_t[:]), pb[t][:], pa_neg[t][:], ALU.add)
+            nc.vector.scalar_tensor_tensor(rb[:], pa_neg[t][:], -0.5, pb[t][:], ALU.mult, ALU.max)
+            if t + 1 < PACK:
+                fetch_pb(t + 1)
+            nc.vector.scalar_tensor_tensor(st[t][:], y[t][:], gm_neg[:, t : t + 1], sig[t], ALU.mult, ALU.mult)
+            nc.vector.tensor_copy(dt[:].indirect(n2_t[:]), rb[:])
+            nc.sync.dma_start(st_copy[t][:], st[t][:])
+            deal_weight_half(nc.scalar.copy, *late_weights[t])
+            nc.scalar.activation(z_planes[:, t, :], dt[:], ACT.Copy, scale=gn_t[:, t : t + 1])
+
+        def quantize_tiles(w_bf, first, last, name, tag=""):
+            return quantize(w_bf[:, first:last].rearrange("p t m j -> p (t m j)"), name, tag)
+
+        w2_first = quantize_tiles(w2_bf, 0, 1, "w2_first")
+        w3_first = quantize_tiles(w3_bf, 0, 1, "w3_first")
+        z_grouped = interleave(nc.scalar.copy, z_planes[:], "z_grouped")
+
+        z2_planes = [
+            keep.tile([P, PACK, HALF], F32, name="z2_planes%d" % u, align_bytes=64, tag="z2_planes%d" % u)
+            for u in range(2)
+        ]
+
+        def fetch_z2(u, t):
+            nc.vector.tensor_tensor(
+                z2_planes[u][:, t, :], st[t][:].indirect(half_of(n4_t, u)), st_copy[t][:, halves[u]], ALU.subtract
+            )
+
+        for t in range(PACK):
+            fetch_z2(0, t)
+        z2_grouped0 = interleave(nc.scalar.copy, z2_planes[0][:], "z2_grouped0")
+        fetch_z2(1, 0)
+        fetch_z2(1, 1)
+        z_q = quantize(z_grouped, "z")
+        fetch_z2(1, 2)
+        z2_q0 = quantize(z2_grouped0, "z2a")
+        fetch_z2(1, 3)
+        z2_grouped1 = interleave(nc.vector.tensor_copy, z2_planes[1][:], "z2_grouped1")
+        z2_q = [z2_q0, quantize(z2_grouped1, "z2b")]
+
+        acc = [psum.tile([P, HALF], F32, name="h_acc0_%d" % u, tag="bank%d" % (PACK * u)) for u in range(2)]
+        mx_pass(acc[0][:], w2_first, 0, z_q, halves[0], True, False)
+        mx_pass(acc[1][:], w2_first, 0, z_q, halves[1], True, False)
+        for u in range(2):
+            mx_pass(acc[u][:], w3_first, 0, z2_q[u], slice(0, HALF), False, True)
+            nc.scalar.copy(h[0][:, halves[u]], acc[u][:])
+
+        late = keep.tile([P, 2, 3 * P], U32, name="late_codes", align_bytes=64, tag="z2_planes1")
+        late_scales = keep.tile([P, 2, 3 * P], U8, name="late_scales", align_bytes=64)
+        for first, last in ((1, 2), (2, 4)):
+            for i, w_bf in enumerate((w2_bf, w3_bf)):
+                cols = slice((first - 1) * P, (last - 1) * P)
+                nc.vector.quantize_mx(
+                    out=late[:, i, cols].bitcast(FP8X4),
+                    scales=late_scales[:, i, cols],
+                    in_=w_bf[:, first:last].rearrange("p t m j -> p (t m j)"),
+                )
+        w2_late = (late[:, 0, :], late_scales[:, 0, :])
+        w3_late = (late[:, 1, :], late_scales[:, 1, :])
+        for t in range(1, PACK):
+            acc_t = psum.tile([P, S], F32, name="h_acc%d" % t, tag="bank%d" % t)
+            for u in range(2):
+                mx_pass(acc_t[:, halves[u]], w2_late, t - 1, z_q, halves[u], True, False)
+                mx_pass(acc_t[:, halves[u]], w3_late, t - 1, z2_q[u], slice(0, HALF), False, True)
+            nc.scalar.copy(h[t], acc_t[:])
+
+        blocks = [slice(b * P, (b + 1) * P) for b in range(S // P)]
+        picked = [keep.tile([P, 2, S], F32, name="picked%d" % t) for t in range(PACK)]
+        weight = [keep.tile([P, 2, S], F32, name="weight%d" % t) for t in range(PACK)]
+        diff = [keep.tile([P, 2, S], F32, name="diff%d" % t) for t in range(PACK)]
+        den_sq = [keep.tile([P, S], F32, name="den_sq%d" % t) for t in range(PACK)]
+        num = [keep.tile([P, S], F32, name="num%d" % t) for t in range(PACK)]
+
+        def fetch(t, a):
+            nc.vector.tensor_copy(picked[t][:, a, :], h_window[t][:].indirect((n5_t, n6_t)[a][:]))
+
+        def weigh(t, sides):
+            count = sides.stop - sides.start
+            nc.vector.tensor_tensor(
+                diff[t][:, sides, :], picked[t][:, sides, :], h[t].unsqueeze(1).to_broadcast([P, count, S]), ALU.subtract
+            )
+            nc.scalar.activation(diff[t][:, sides, :], diff[t][:, sides, :], ACT.Square)
+            nc.scalar.activation(weight[t][:, sides, :], diff[t][:, sides, :], ACT.Exp, scale=-0.5)
+
+        def denominator(t):
+            sum_t = psum.tile([P, S], F32, name="sum%d" % t, tag="bank%d" % (PACK + t))
+            for b in blocks:
+                for a in range(2):
+                    nc.tensor.matmul(
+                        sum_t[:, b], weight[t][:, a, b], ident[:], start=(a == 0), stop=(a == 1), is_transpose=True
+                    )
+            nc.scalar.activation(den_sq[t][:], sum_t[:], ACT.Square, bias=0.5)
+
+        def products(t):
+            nc.vector.tensor_tensor(picked[t][:], picked[t][:], weight[t][:], ALU.mult)
+
+        def numerator(t):
+            nc.vector.tensor_tensor(num[t][:], picked[t][:, 0, :], picked[t][:, 1, :], ALU.add)
+
+        out_rows = out.rearrange("(p t) j -> p t j", t=PACK)
+
+        def finish(t):
+            inv_t = keep.tile([P, S], F32, name="inv%d" % t)
+            nc.scalar.activation(inv_t[:], den_sq[t][:], ACT.Abs_reciprocal_sqrt)
+            inv_back = psum.tile([P, S], F32, name="inv_back%d" % t, tag="bank%d" % t)
+            for b in blocks:
+                nc.tensor.transpose(inv_back[:, b], inv_t[:, b], ident[:])
+            nc.vector.tensor_tensor(num[t][:], num[t][:], inv_back[:], ALU.mult)
+            nc.sync.dma_start(out_rows[:, t, :], num[t][:])
+
+        last = PACK - 1
+        fetch(0, 0)
+        fetch(0, 1)
+        for t in range(1, PACK):
+            fetch(t, 0)
+            weigh(t - 1, slice(0, 2))
+            denominator(t - 1)
+            if t == last:
+                weigh(t, slice(0, 1))
+            fetch(t, 1)
+        products(0)
+        weigh(last, slice(1, 2))
+        denominator(last)
+        for t in range(1, PACK):
+            products(t)
+            numerator(t - 1)
+        finish(0)
+        numerator(last)
+        for t in range(1, PACK):
+            finish(t)

@@ -144,30 +144,32 @@ def tile_picked_joinlifthopgkern_none_p_kernel(
         st = [keep.tile([P, S], F32, name="st%d" % t) for t in range(PACK)]
         st_copy = [keep.tile([P, S], F32, name="st_copy%d" % t) for t in range(PACK)]
 
-        def fetch_pa(t):
-            nc.vector.tensor_scalar(pa_neg[t][:], y[t][:].indirect(n1_t[:]), -1.0, 0.0, ALU.mult, ALU.add)
-
-        def fetch_pb(t):
-            nc.vector.tensor_copy(pb[t][:], y[t][:].indirect(n2_t[:]))
-
-        fetch_pa(0)
-        fetch_pb(0)
+        ra = [keep.tile([P, HALF], F32, name="ra%d" % t) for t in range(PACK)]
+        rb = [keep.tile([P, HALF], F32, name="rb%d" % t) for t in range(PACK)]
+        dt = [keep.tile([P, S], F32, name="dt%d" % t) for t in range(PACK)]
         for t in range(PACK):
+            nc.vector.tensor_scalar(pa_neg[t][:], y[t][:].indirect(n1_t[:]), -0.5, 0.0, ALU.mult, ALU.add)
+            nc.vector.tensor_copy(pb[t][:], y[t][:].indirect(n2_t[:]))
+            nc.gpsimd.tensor_tensor(pb[t][:], pb[t][:], pa_neg[t][:], ALU.add)
+            nc.gpsimd.tensor_tensor(ra[t][:], pb[t][:], pa_neg[t][:], ALU.add)
+            nc.scalar.activation(rb[t][:], pb[t][:], ACT.Relu)
+            nc.gpsimd.tensor_tensor(rb[t][:], rb[t][:], pa_neg[t][:], ALU.subtract)
             for u in range(2):
                 nc.scalar.activation(sig[t][:, halves[u]], y[t][:].indirect(half_of(n3_t, u)), ACT.Sigmoid)
-            rb = keep.tile([P, HALF], F32, name="rb%d" % t)
-            dt = keep.tile([P, S], F32, name="dt%d" % t)
+
+        def put(t, values, list_tile):
+            nc.vector.tensor_copy(dt[t][:].indirect(list_tile[:]), values[t][:])
+
+        put(0, ra, n1_t)
+        for t in range(PACK):
             if t + 1 < PACK:
-                fetch_pa(t + 1)
-            nc.vector.tensor_tensor(dt[:].indirect(n1_t[:]), pb[t][:], pa_neg[t][:], ALU.add)
-            nc.vector.scalar_tensor_tensor(rb[:], pa_neg[t][:], -0.5, pb[t][:], ALU.mult, ALU.max)
-            if t + 1 < PACK:
-                fetch_pb(t + 1)
-            nc.vector.scalar_tensor_tensor(st[t][:], y[t][:], gm_neg[:, t : t + 1], sig[t], ALU.mult, ALU.mult)
-            nc.vector.tensor_copy(dt[:].indirect(n2_t[:]), rb[:])
+                put(t + 1, ra, n1_t)
+            put(t, rb, n2_t)
+            nc.scalar.activation(st[t][:], y[t][:], ACT.Copy, scale=gm_neg[:, t : t + 1])
+            nc.gpsimd.tensor_tensor(st[t][:], st[t][:], sig[t], ALU.mult)
             nc.sync.dma_start(st_copy[t][:], st[t][:])
             deal_weight_half(nc.scalar.copy, *late_weights[t])
-            nc.scalar.activation(z_planes[:, t, :], dt[:], ACT.Copy, scale=gn_t[:, t : t + 1])
+            nc.scalar.activation(z_planes[:, t, :], dt[t][:], ACT.Copy, scale=gn_t[:, t : t + 1])
 
         def quantize_tiles(w_bf, first, last, name, tag=""):
             return quantize(w_bf[:, first:last].rearrange("p t m j -> p (t m j)"), name, tag)
@@ -198,6 +200,8 @@ def tile_picked_joinlifthopgkern_none_p_kernel(
         z2_grouped1 = interleave(nc.vector.tensor_copy, z2_planes[1][:], "z2_grouped1")
         z2_q = [z2_q0, quantize(z2_grouped1, "z2b")]
 
+        warm_exp = keep.tile([P, 1], F32, name="warm_exp")
+        nc.scalar.activation(warm_exp[:], z2_grouped0[:, 0:1], ACT.Exp, scale=0.0)
         acc = [psum.tile([P, HALF], F32, name="h_acc0_%d" % u, tag="bank%d" % (PACK * u)) for u in range(2)]
         mx_pass(acc[0][:], w2_first, 0, z_q, halves[0], True, False)
         mx_pass(acc[1][:], w2_first, 0, z_q, halves[1], True, False)
@@ -234,13 +238,10 @@ def tile_picked_joinlifthopgkern_none_p_kernel(
         def fetch(t, a):
             nc.vector.tensor_copy(picked[t][:, a, :], h_window[t][:].indirect((n5_t, n6_t)[a][:]))
 
-        def weigh(t, sides):
-            count = sides.stop - sides.start
-            nc.vector.tensor_tensor(
-                diff[t][:, sides, :], picked[t][:, sides, :], h[t].unsqueeze(1).to_broadcast([P, count, S]), ALU.subtract
-            )
-            nc.scalar.activation(diff[t][:, sides, :], diff[t][:, sides, :], ACT.Square)
-            nc.scalar.activation(weight[t][:, sides, :], diff[t][:, sides, :], ACT.Exp, scale=-0.5)
+        def weigh(t, a, engine):
+            engine.tensor_tensor(diff[t][:, a, :], picked[t][:, a, :], h[t], ALU.subtract)
+            nc.scalar.activation(diff[t][:, a, :], diff[t][:, a, :], ACT.Square)
+            nc.scalar.activation(weight[t][:, a, :], diff[t][:, a, :], ACT.Exp, scale=-0.5)
 
         def denominator(t):
             sum_t = psum.tile([P, S], F32, name="sum%d" % t, tag="bank%d" % (PACK + t))
@@ -269,18 +270,14 @@ def tile_picked_joinlifthopgkern_none_p_kernel(
             nc.sync.dma_start(out_rows[:, t, :], num[t][:])
 
         last = PACK - 1
-        fetch(0, 0)
-        fetch(0, 1)
-        for t in range(1, PACK):
-            fetch(t, 0)
-            weigh(t - 1, slice(0, 2))
-            denominator(t - 1)
-            if t == last:
-                weigh(t, slice(0, 1))
-            fetch(t, 1)
-        products(0)
-        weigh(last, slice(1, 2))
+        for t in range(PACK):
+            for a in range(2):
+                fetch(t, a)
+                weigh(t, a, nc.vector if (t, a) == (last, 1) else nc.gpsimd)
+                if a == 0 and t > 0:
+                    denominator(t - 1)
         denominator(last)
+        products(0)
         for t in range(1, PACK):
             products(t)
             numerator(t - 1)

@@ -39,16 +39,16 @@ def tile_picked_joinlifthopgkern_none_p_kernel(
             cols = HALF // 16
             return list_tile[:, u * cols : (u + 1) * cols]
 
-        def load_weight_half(w, u, name):
-            raw = keep.tile([P, PACK, HALF], F32, name=name)
-            nc.sync.dma_start(raw[:], w.rearrange("(p j) c -> p j c", j=PACK)[:, :, u * HALF : (u + 1) * HALF])
+        def load_weight(w, name):
+            raw = keep.tile([P, PACK, S], F32, name=name)
+            nc.sync.dma_start(raw[:], w.rearrange("(p j) c -> p j c", j=PACK))
             return raw
 
         def deal_weight_half(copy, grouped, raw, u):
             m_half = slice(u * P // 2, (u + 1) * P // 2)
             copy(
                 grouped[:, :, m_half, :].rearrange("p t m j -> p m j t"),
-                raw[:].rearrange("p j (m t) -> p m j t", t=PACK),
+                raw[:, :, halves[u]].rearrange("p j (m t) -> p m j t", t=PACK),
             )
 
         def quantize(grouped, name, tag=""):
@@ -58,9 +58,9 @@ def tile_picked_joinlifthopgkern_none_p_kernel(
             nc.vector.quantize_mx(out=codes[:].bitcast(FP8X4), scales=scales[:], in_=grouped)
             return codes, scales
 
-        def interleave(copy, planes, name):
+        def interleave(copy, planes, name, tag=""):
             width = planes.shape[2]
-            grouped = keep.tile([P, width, PACK], BF16, name=name, align_bytes=64)
+            grouped = keep.tile([P, width, PACK], BF16, name=name, align_bytes=64, tag=tag)
             copy(
                 grouped[:].rearrange("p (c i) t -> p c t i", i=4),
                 planes.rearrange("p t (c i) -> p c t i", i=4),
@@ -91,7 +91,7 @@ def tile_picked_joinlifthopgkern_none_p_kernel(
         nc.gpsimd.memset(warm[:, 0:1], 0.0)
         nc.scalar.activation(warm[:, 1:2], warm[:, 0:1], ACT.Sigmoid)
         offs_t = load_list(offs, "offs")
-        w1_raw = [load_weight_half(w1, u, "w1_raw%d" % u) for u in range(2)]
+        w1_raw = load_weight(w1, "w1_raw")
         xw_all = keep.tile([P, T], I32, name="xw_all")
         nc.sync.dma_start(xw_all[:], x_words[0].rearrange("p n t -> p (n t)").bitcast(I32))
         n1_t, n2_t, n3_t = load_list(n1, "n1"), load_list(n2, "n2"), load_list(n3, "n3")
@@ -99,44 +99,39 @@ def tile_picked_joinlifthopgkern_none_p_kernel(
         nc.sync.dma_start(gn_t[:], gn.rearrange("(p t) o -> p (t o)", t=PACK))
         gm_t = keep.tile([P, PACK], F32, name="gm_t")
         nc.sync.dma_start(gm_t[:], gm.rearrange("(p t) o -> p (t o)", t=PACK))
-        w2_raw = [load_weight_half(w2, u, "w2_raw%d" % u) for u in range(2)]
-        w3_raw = [load_weight_half(w3, u, "w3_raw%d" % u) for u in range(2)]
+        w2_raw = load_weight(w2, "w2_raw")
+        w3_raw = load_weight(w3, "w3_raw")
         n4_t, n5_t, n6_t = load_list(n4, "n4"), load_list(n5, "n5"), load_list(n6, "n6")
 
         ident = keep.tile([P, P], F32, name="ident")
         make_identity(nc, ident[:])
-        gm_neg = keep.tile([P, PACK], F32, name="gm_neg")
-        nc.gpsimd.tensor_scalar(gm_neg[:], gm_t[:], -1.0, 0.0, ALU.mult, ALU.add)
 
         xq_scales = keep.tile([P, S], U8, name="xq_scales", align_bytes=64)
         nc.vector.tensor_copy(xq_scales[:], xs_all[:].indirect(offs_t[:]))
         w1_bf = keep.tile([P, PACK, P, PACK], BF16, name="w1_bf", align_bytes=64)
-        deal_weight_half(nc.scalar.copy, w1_bf, w1_raw[0], 0)
-        deal_weight_half(nc.vector.tensor_copy, w1_bf, w1_raw[1], 1)
-        w1_q = quantize(w1_bf[:].rearrange("p t m j -> p (t m j)"), "w1")
+        deal_weight_half(nc.scalar.copy, w1_bf, w1_raw, 0)
+        deal_weight_half(nc.vector.tensor_copy, w1_bf, w1_raw, 1)
+        w1_q = quantize(w1_bf[:].rearrange("p t m j -> p (t m j)"), "w1", "w1_codes")
 
-        xq_words = keep.tile([P, S], U32, name="xq_words", align_bytes=64)
+        xq_words = keep.tile([P, S], U32, name="xq_words", align_bytes=64, tag="xq_words")
         for u in range(2):
             nc.vector.tensor_copy(xq_words[:, halves[u]], xw_all[:].bitcast(U32).indirect(half_of(offs_t, u)))
         xq = (xq_words, xq_scales)
 
         y = []
         for t in range(PACK):
-            acc = psum.tile([P, S], F32, name="y_acc%d" % t, tag="bank%d" % t)
-            if t == 0:
-                for u in range(2):
-                    mx_pass(acc[:, halves[u]], w1_q, t, xq, halves[u], True, True)
-            else:
-                mx_pass(acc[:], w1_q, t, xq, slice(0, S), True, True)
             y_t = keep.tile([P, S], F32, name="y%d" % t)
-            nc.scalar.copy(y_t[:], acc[:])
+            for u, cols in enumerate(halves if t == 0 else [slice(0, S)]):
+                acc = psum.tile([P, cols.stop - cols.start], F32, name="y_acc%d_%d" % (t, u), tag="bank%d" % (t + PACK * u))
+                mx_pass(acc[:], w1_q, t, xq, cols, True, True)
+                nc.scalar.copy(y_t[:, cols], acc[:])
             y.append(y_t)
 
-        w2_bf = keep.tile([P, PACK, P, PACK], BF16, name="w2_bf", align_bytes=64)
-        w3_bf = keep.tile([P, PACK, P, PACK], BF16, name="w3_bf", align_bytes=64)
-        late_weights = [(w2_bf, w2_raw[0], 0), (w2_bf, w2_raw[1], 1), (w3_bf, w3_raw[0], 0), (w3_bf, w3_raw[1], 1)]
-        z_planes = keep.tile([P, PACK, S], BF16, name="z_planes")
-        h_window = [keep.tile([P, 2 * S], F32, name="h_window%d" % t) for t in range(PACK)]
+        w2_bf = keep.tile([P, PACK, P, PACK], BF16, name="w2_bf", align_bytes=64, tag="w1_codes")
+        w3_bf = keep.tile([P, PACK, P, PACK], BF16, name="w3_bf", align_bytes=64, tag="xq_words")
+        late_weights = [(w2_bf, w2_raw, 0), (w2_bf, w2_raw, 1), (w3_bf, w3_raw, 0), (w3_bf, w3_raw, 1)]
+        z_planes = keep.tile([P, PACK, S], BF16, name="z_planes", align_bytes=64, tag="z_planes")
+        h_window = [keep.tile([P, 2 * S], F32, name="h_window%d" % t, tag="h_window%d" % t) for t in range(PACK)]
         h = [w[:, 0:S] for w in h_window]
         sig = [w[:, S : 2 * S] for w in h_window]
         pa_neg = [keep.tile([P, HALF], F32, name="pa_neg%d" % t) for t in range(PACK)]
@@ -144,42 +139,48 @@ def tile_picked_joinlifthopgkern_none_p_kernel(
         st = [keep.tile([P, S], F32, name="st%d" % t) for t in range(PACK)]
         st_copy = [keep.tile([P, S], F32, name="st_copy%d" % t) for t in range(PACK)]
 
-        ra = [keep.tile([P, HALF], F32, name="ra%d" % t) for t in range(PACK)]
-        rb = [keep.tile([P, HALF], F32, name="rb%d" % t) for t in range(PACK)]
-        dt = [keep.tile([P, S], F32, name="dt%d" % t) for t in range(PACK)]
+        ra = [keep.tile([P, HALF], F32, name="ra%d" % t, align_bytes=64, tag="ra%d" % t) for t in range(PACK)]
+        rb = [keep.tile([P, HALF], F32, name="rb%d" % t, align_bytes=64, tag="rb%d" % t) for t in range(PACK)]
+        dt = [keep.tile([P, S], F32, name="dt%d" % t, align_bytes=64, tag="dt%d" % t) for t in range(PACK)]
+        last = PACK - 1
+
         for t in range(PACK):
             nc.vector.tensor_scalar(pa_neg[t][:], y[t][:].indirect(n1_t[:]), -0.5, 0.0, ALU.mult, ALU.add)
             nc.vector.tensor_copy(pb[t][:], y[t][:].indirect(n2_t[:]))
             nc.gpsimd.tensor_tensor(pb[t][:], pb[t][:], pa_neg[t][:], ALU.add)
             nc.gpsimd.tensor_tensor(ra[t][:], pb[t][:], pa_neg[t][:], ALU.add)
-            nc.scalar.activation(rb[t][:], pb[t][:], ACT.Relu)
-            nc.gpsimd.tensor_tensor(rb[t][:], rb[t][:], pa_neg[t][:], ALU.subtract)
+        for t in range(PACK):
+            nc.vector.tensor_copy(dt[t][:].indirect(n1_t[:]), ra[t][:])
+
+        for t in range(PACK):
             for u in range(2):
                 nc.scalar.activation(sig[t][:, halves[u]], y[t][:].indirect(half_of(n3_t, u)), ACT.Sigmoid)
-
-        def put(t, values, list_tile):
-            nc.vector.tensor_copy(dt[t][:].indirect(list_tile[:]), values[t][:])
-
-        put(0, ra, n1_t)
-        for t in range(PACK):
-            if t + 1 < PACK:
-                put(t + 1, ra, n1_t)
-            put(t, rb, n2_t)
-            nc.scalar.activation(st[t][:], y[t][:], ACT.Copy, scale=gm_neg[:, t : t + 1])
+            nc.scalar.activation(rb[t][:], pb[t][:], ACT.Relu)
+            nc.gpsimd.tensor_tensor(rb[t][:], rb[t][:], pa_neg[t][:], ALU.subtract)
+            nc.scalar.activation(st[t][:], y[t][:], ACT.Copy, scale=gm_t[:, t : t + 1])
             nc.gpsimd.tensor_tensor(st[t][:], st[t][:], sig[t], ALU.mult)
             nc.sync.dma_start(st_copy[t][:], st[t][:])
-            deal_weight_half(nc.scalar.copy, *late_weights[t])
+        for weights in late_weights:
+            deal_weight_half(nc.scalar.copy, *weights)
+        for t in range(PACK):
+            nc.vector.tensor_copy(dt[t][:].indirect(n2_t[:]), rb[t][:])
             nc.scalar.activation(z_planes[:, t, :], dt[t][:], ACT.Copy, scale=gn_t[:, t : t + 1])
+
+        def negate_on_scalar(dst, src):
+            nc.scalar.activation(dst, src, ACT.Copy, scale=-1.0)
+
+        def negate_on_vector(dst, src):
+            nc.vector.tensor_scalar(dst, src, -1.0, None, ALU.mult)
 
         def quantize_tiles(w_bf, first, last, name, tag=""):
             return quantize(w_bf[:, first:last].rearrange("p t m j -> p (t m j)"), name, tag)
 
-        w2_first = quantize_tiles(w2_bf, 0, 1, "w2_first")
-        w3_first = quantize_tiles(w3_bf, 0, 1, "w3_first")
-        z_grouped = interleave(nc.scalar.copy, z_planes[:], "z_grouped")
+        w2_q = quantize_tiles(w2_bf, 0, PACK, "w2", "rb%d" % (last - 1))
+        w3_first = quantize_tiles(w3_bf, 0, 1, "w3_first", "dt%d" % (last - 1))
+        z_grouped = interleave(nc.scalar.copy, z_planes[:], "z_grouped", "z_grouped")
 
         z2_planes = [
-            keep.tile([P, PACK, HALF], F32, name="z2_planes%d" % u, align_bytes=64, tag="z2_planes%d" % u)
+            keep.tile([P, PACK, HALF], F32, name="z2_planes%d" % u, align_bytes=64, tag=("rb%d" % last, "z_grouped")[u])
             for u in range(2)
         ]
 
@@ -190,56 +191,52 @@ def tile_picked_joinlifthopgkern_none_p_kernel(
 
         for t in range(PACK):
             fetch_z2(0, t)
-        z2_grouped0 = interleave(nc.scalar.copy, z2_planes[0][:], "z2_grouped0")
-        fetch_z2(1, 0)
-        fetch_z2(1, 1)
+        z2_grouped0 = interleave(negate_on_scalar, z2_planes[0][:], "z2_grouped0", "z_planes")
         z_q = quantize(z_grouped, "z")
-        fetch_z2(1, 2)
+        for t in range(PACK):
+            fetch_z2(1, t)
         z2_q0 = quantize(z2_grouped0, "z2a")
-        fetch_z2(1, 3)
-        z2_grouped1 = interleave(nc.vector.tensor_copy, z2_planes[1][:], "z2_grouped1")
+        z2_grouped1 = interleave(negate_on_vector, z2_planes[1][:], "z2_grouped1", "z_planes")
         z2_q = [z2_q0, quantize(z2_grouped1, "z2b")]
 
         warm_exp = keep.tile([P, 1], F32, name="warm_exp")
         nc.scalar.activation(warm_exp[:], z2_grouped0[:, 0:1], ACT.Exp, scale=0.0)
-        acc = [psum.tile([P, HALF], F32, name="h_acc0_%d" % u, tag="bank%d" % (PACK * u)) for u in range(2)]
-        mx_pass(acc[0][:], w2_first, 0, z_q, halves[0], True, False)
-        mx_pass(acc[1][:], w2_first, 0, z_q, halves[1], True, False)
-        for u in range(2):
-            mx_pass(acc[u][:], w3_first, 0, z2_q[u], slice(0, HALF), False, True)
-            nc.scalar.copy(h[0][:, halves[u]], acc[u][:])
-
-        late = keep.tile([P, 2, 3 * P], U32, name="late_codes", align_bytes=64, tag="z2_planes1")
-        late_scales = keep.tile([P, 2, 3 * P], U8, name="late_scales", align_bytes=64)
-        for first, last in ((1, 2), (2, 4)):
-            for i, w_bf in enumerate((w2_bf, w3_bf)):
-                cols = slice((first - 1) * P, (last - 1) * P)
-                nc.vector.quantize_mx(
-                    out=late[:, i, cols].bitcast(FP8X4),
-                    scales=late_scales[:, i, cols],
-                    in_=w_bf[:, first:last].rearrange("p t m j -> p (t m j)"),
-                )
-        w2_late = (late[:, 0, :], late_scales[:, 0, :])
-        w3_late = (late[:, 1, :], late_scales[:, 1, :])
-        for t in range(1, PACK):
-            acc_t = psum.tile([P, S], F32, name="h_acc%d" % t, tag="bank%d" % t)
+        acc = [
+            [psum.tile([P, HALF], F32, name="h_acc%d_%d" % (t, u), tag="bank%d" % (t + PACK * u)) for u in range(2)]
+            for t in range(PACK)
+        ]
+        for t in range(PACK):
             for u in range(2):
-                mx_pass(acc_t[:, halves[u]], w2_late, t - 1, z_q, halves[u], True, False)
-                mx_pass(acc_t[:, halves[u]], w3_late, t - 1, z2_q[u], slice(0, HALF), False, True)
-            nc.scalar.copy(h[t], acc_t[:])
+                mx_pass(acc[t][u][:], w2_q, t, z_q, halves[u], True, False)
+
+        def close(t, weights, column_block):
+            for u in range(2):
+                mx_pass(acc[t][u][:], weights, column_block, z2_q[u], slice(0, HALF), False, True)
+                nc.scalar.copy(h[t][:, halves[u]], acc[t][u][:])
+
+        close(0, w3_first, 0)
+        late = keep.tile([P, 3 * P], U32, name="late_codes", align_bytes=64, tag="z_grouped")
+        late_scales = keep.tile([P, 3 * P], U8, name="late_scales", align_bytes=64)
+        for first, stop in ((1, 2), (2, 4)):
+            cols = slice((first - 1) * P, (stop - 1) * P)
+            nc.vector.quantize_mx(
+                out=late[:, cols].bitcast(FP8X4),
+                scales=late_scales[:, cols],
+                in_=w3_bf[:, first:stop].rearrange("p t m j -> p (t m j)"),
+            )
+        for t in range(1, PACK):
+            close(t, (late, late_scales), t - 1)
 
         blocks = [slice(b * P, (b + 1) * P) for b in range(S // P)]
-        picked = [keep.tile([P, 2, S], F32, name="picked%d" % t) for t in range(PACK)]
+        picked = [keep.tile([P, 2, S], F32, name="picked%d" % t, tag="picked%d" % t) for t in range(PACK)]
         weight = [keep.tile([P, 2, S], F32, name="weight%d" % t) for t in range(PACK)]
         diff = [keep.tile([P, 2, S], F32, name="diff%d" % t) for t in range(PACK)]
         den_sq = [keep.tile([P, S], F32, name="den_sq%d" % t) for t in range(PACK)]
-        num = [keep.tile([P, S], F32, name="num%d" % t) for t in range(PACK)]
 
         def fetch(t, a):
             nc.vector.tensor_copy(picked[t][:, a, :], h_window[t][:].indirect((n5_t, n6_t)[a][:]))
 
-        def weigh(t, a, engine):
-            engine.tensor_tensor(diff[t][:, a, :], picked[t][:, a, :], h[t], ALU.subtract)
+        def weigh(t, a):
             nc.scalar.activation(diff[t][:, a, :], diff[t][:, a, :], ACT.Square)
             nc.scalar.activation(weight[t][:, a, :], diff[t][:, a, :], ACT.Exp, scale=-0.5)
 
@@ -252,36 +249,53 @@ def tile_picked_joinlifthopgkern_none_p_kernel(
                     )
             nc.scalar.activation(den_sq[t][:], sum_t[:], ACT.Square, bias=0.5)
 
+        prod, num = [], []
+
         def products(t):
-            nc.vector.tensor_tensor(picked[t][:], picked[t][:], weight[t][:], ALU.mult)
+            prod_t = keep.tile([P, 2, S], F32, name="prod%d" % t, tag="h_window%d" % ((t + 2) % PACK))
+            nc.vector.tensor_tensor(prod_t[:], picked[t][:], weight[t][:], ALU.mult)
+            prod.append(prod_t)
 
         def numerator(t):
-            nc.vector.tensor_tensor(num[t][:], picked[t][:, 0, :], picked[t][:, 1, :], ALU.add)
+            num_t = keep.tile([P, S], F32, name="num%d" % t, tag="picked%d" % ((t + 1) % PACK))
+            nc.vector.tensor_tensor(num_t[:], prod[t][:, 0, :], prod[t][:, 1, :], ALU.add)
+            num.append(num_t)
 
         out_rows = out.rearrange("(p t) j -> p t j", t=PACK)
 
-        def finish(t):
-            inv_t = keep.tile([P, S], F32, name="inv%d" % t)
-            nc.scalar.activation(inv_t[:], den_sq[t][:], ACT.Abs_reciprocal_sqrt)
-            inv_back = psum.tile([P, S], F32, name="inv_back%d" % t, tag="bank%d" % t)
-            for b in blocks:
-                nc.tensor.transpose(inv_back[:, b], inv_t[:, b], ident[:])
-            nc.vector.tensor_tensor(num[t][:], num[t][:], inv_back[:], ALU.mult)
-            nc.sync.dma_start(out_rows[:, t, :], num[t][:])
+        def finish(t, cols, bank):
+            width = cols.stop - cols.start
+            inv = keep.tile([P, width], F32, name="inv%d" % bank)
+            nc.scalar.activation(inv[:], den_sq[t][:, cols], ACT.Abs_reciprocal_sqrt)
+            inv_back = psum.tile([P, width], F32, name="inv_back%d" % bank, tag="bank%d" % bank)
+            for b in blocks[: width // P]:
+                nc.tensor.transpose(inv_back[:, b], inv[:, b], ident[:])
+            nc.vector.tensor_tensor(num[t][:, cols], num[t][:, cols], inv_back[:], ALU.mult)
+            nc.sync.dma_start(out_rows[:, t, cols], num[t][:, cols])
 
-        last = PACK - 1
-        for t in range(PACK):
+        for t in range(last):
             for a in range(2):
                 fetch(t, a)
-                weigh(t, a, nc.vector if (t, a) == (last, 1) else nc.gpsimd)
+                nc.gpsimd.tensor_tensor(diff[t][:, a, :], picked[t][:, a, :], h[t], ALU.subtract)
+                weigh(t, a)
                 if a == 0 and t > 0:
                     denominator(t - 1)
+        for a in range(2):
+            fetch(last, a)
+        nc.vector.tensor_tensor(
+            diff[last][:], picked[last][:], h[last].unsqueeze(1).to_broadcast([P, 2, S]), ALU.subtract
+        )
+        weigh(last, 0)
+        denominator(last - 1)
+        weigh(last, 1)
         denominator(last)
         products(0)
         for t in range(1, PACK):
             products(t)
             numerator(t - 1)
-        finish(0)
+        finish(0, slice(0, S), 0)
         numerator(last)
-        for t in range(1, PACK):
-            finish(t)
+        for t in range(1, last):
+            finish(t, slice(0, S), t)
+        for u in range(2):
+            finish(last, halves[u], last + u)

@@ -14,10 +14,14 @@ ALU = mybir.AluOpType
 ACT = mybir.ActivationFunctionType
 
 P = 128
-PACK = 4
+PLANES = 4
+LAST = PLANES - 1
 T = 2048
 S = 512
 HALF = S // 2
+LIST_ROWS = 16
+LINE = 4
+ALIGN = 64
 FLOPS = 3 * 2 * 512 * 512 * 512
 
 
@@ -25,61 +29,77 @@ def tile_picked_joinlifthopgkern_none_p_kernel(
     tc, x_words, x_scales, w1, gn, gm, w2, w3, offs, n1, n2, n3, n4, n5, n6, out
 ):
     nc = tc.nc
+    halves = [slice(0, HALF), slice(HALF, S)]
+    blocks = [slice(b * P, (b + 1) * P) for b in range(S // P)]
+
     with ExitStack() as ctx:
         lists = ctx.enter_context(tc.tile_pool(name="lists", bufs=1))
         keep = ctx.enter_context(tc.tile_pool(name="keep", bufs=1))
         psum = ctx.enter_context(tc.psum_pool(name="psum", bufs=1))
 
-        def load_list(src, name):
-            tile = lists.tile([P, src.shape[1]], U16, name=name)
-            nc.sync.dma_start(tile[:], src)
+        def per_plane(name, shape, align=None):
+            return [
+                keep.tile(shape, F32, name="%s%d" % (name, t), tag="%s%d" % (name, t), align_bytes=align)
+                for t in range(PLANES)
+            ]
+
+        def bank(number, width, name):
+            return psum.tile([P, width], F32, name=name, tag="bank%d" % number)
+
+        def load_list(source, name):
+            tile = lists.tile([P, source.shape[1]], U16, name=name)
+            nc.sync.dma_start(tile[:], source)
             return tile
 
         def half_of(list_tile, u):
-            cols = HALF // 16
-            return list_tile[:, u * cols : (u + 1) * cols]
+            columns = HALF // LIST_ROWS
+            return list_tile[:, u * columns : (u + 1) * columns]
 
         def load_weight(w, name):
-            raw = keep.tile([P, PACK, S], F32, name=name)
-            nc.sync.dma_start(raw[:], w.rearrange("(p j) c -> p j c", j=PACK))
+            raw = keep.tile([P, PLANES, S], F32, name=name)
+            nc.sync.dma_start(raw[:], w.rearrange("(p j) c -> p j c", j=PLANES))
             return raw
 
-        def deal_weight_half(copy, grouped, raw, u):
+        def load_gain(gain, name):
+            tile = keep.tile([P, PLANES], F32, name=name)
+            nc.sync.dma_start(tile[:], gain.rearrange("(p t) o -> p (t o)", t=PLANES))
+            return tile
+
+        def deal_half(copy, dealt, raw, u):
             m_half = slice(u * P // 2, (u + 1) * P // 2)
             copy(
-                grouped[:, :, m_half, :].rearrange("p t m j -> p m j t"),
-                raw[:, :, halves[u]].rearrange("p j (m t) -> p m j t", t=PACK),
+                dealt[:, :, m_half, :].rearrange("p t m j -> p m j t"),
+                raw[:, :, halves[u]].rearrange("p j (m t) -> p m j t", t=PLANES),
             )
 
-        def quantize(grouped, name, tag=""):
-            width = grouped.shape[1] // PACK
-            codes = keep.tile([P, width], U32, name=name + "_codes", align_bytes=64, tag=tag)
-            scales = keep.tile([P, width], U8, name=name + "_scales", align_bytes=64)
-            nc.vector.quantize_mx(out=codes[:].bitcast(FP8X4), scales=scales[:], in_=grouped)
-            return codes, scales
-
-        def interleave(copy, planes, name, tag=""):
-            width = planes.shape[2]
-            grouped = keep.tile([P, width, PACK], BF16, name=name, align_bytes=64, tag=tag)
+        def interleave(copy, planes, name, tag):
+            grouped = keep.tile([P, planes.shape[2], PLANES], BF16, name=name, align_bytes=ALIGN, tag=tag)
             copy(
-                grouped[:].rearrange("p (c i) t -> p c t i", i=4),
-                planes.rearrange("p t (c i) -> p c t i", i=4),
+                grouped[:].rearrange("p (c i) t -> p c t i", i=LINE),
+                planes.rearrange("p t (c i) -> p c t i", i=LINE),
             )
             return grouped[:].rearrange("p c t -> p (c t)")
 
-        def mx_pass(acc, weights, t, moving, cols, start, stop):
-            rows = slice(t * P, (t + 1) * P)
+        def quantize(grouped, name, tag=""):
+            width = grouped.shape[1] // PLANES
+            codes = keep.tile([P, width], U32, name=name + "_codes", align_bytes=ALIGN, tag=tag)
+            scales = keep.tile([P, width], U8, name=name + "_scales", align_bytes=ALIGN)
+            nc.vector.quantize_mx(out=codes[:].bitcast(FP8X4), scales=scales[:], in_=grouped)
+            return codes, scales
+
+        def dealt_planes(dealt, first, stop):
+            return dealt[:, first:stop].rearrange("p t m j -> p (t m j)")
+
+        def mx_pass(acc, weights, block, moving, cols, start, stop):
             nc.tensor.matmul_mx(
                 out=acc,
-                lhsT=weights[0][:, rows].bitcast(FP8X4),
-                lhsT_scale=weights[1][:, rows],
+                lhsT=weights[0][:, blocks[block]].bitcast(FP8X4),
+                lhsT_scale=weights[1][:, blocks[block]],
                 rhs=moving[0][:, cols].bitcast(FP8X4),
                 rhs_scale=moving[1][:, cols],
                 start=start,
                 stop=stop,
             )
-
-        halves = [slice(u * HALF, (u + 1) * HALF) for u in range(2)]
 
         xs_all = keep.tile([P, T], U8, name="xs_all")
         nc.gpsimd.memset(xs_all[:].bitcast(I32), 0)
@@ -95,76 +115,89 @@ def tile_picked_joinlifthopgkern_none_p_kernel(
         xw_all = keep.tile([P, T], I32, name="xw_all")
         nc.sync.dma_start(xw_all[:], x_words[0].rearrange("p n t -> p (n t)").bitcast(I32))
         n1_t, n2_t, n3_t = load_list(n1, "n1"), load_list(n2, "n2"), load_list(n3, "n3")
-        gn_t = keep.tile([P, PACK], F32, name="gn_t")
-        nc.sync.dma_start(gn_t[:], gn.rearrange("(p t) o -> p (t o)", t=PACK))
-        gm_t = keep.tile([P, PACK], F32, name="gm_t")
-        nc.sync.dma_start(gm_t[:], gm.rearrange("(p t) o -> p (t o)", t=PACK))
-        w2_raw = load_weight(w2, "w2_raw")
-        w3_raw = load_weight(w3, "w3_raw")
+        gn_t, gm_t = load_gain(gn, "gn_t"), load_gain(gm, "gm_t")
+        w2_raw, w3_raw = load_weight(w2, "w2_raw"), load_weight(w3, "w3_raw")
         n4_t, n5_t, n6_t = load_list(n4, "n4"), load_list(n5, "n5"), load_list(n6, "n6")
 
         ident = keep.tile([P, P], F32, name="ident")
         make_identity(nc, ident[:])
 
-        xq_scales = keep.tile([P, S], U8, name="xq_scales", align_bytes=64)
+        xq_scales = keep.tile([P, S], U8, name="xq_scales", align_bytes=ALIGN)
         nc.vector.tensor_copy(xq_scales[:], xs_all[:].indirect(offs_t[:]))
-        w1_bf = keep.tile([P, PACK, P, PACK], BF16, name="w1_bf", align_bytes=64)
-        deal_weight_half(nc.scalar.copy, w1_bf, w1_raw, 0)
-        deal_weight_half(nc.vector.tensor_copy, w1_bf, w1_raw, 1)
-        w1_q = quantize(w1_bf[:].rearrange("p t m j -> p (t m j)"), "w1", "w1_codes")
+        w1_dealt = keep.tile([P, PLANES, P, PLANES], BF16, name="w1_dealt", align_bytes=ALIGN)
+        deal_half(nc.scalar.copy, w1_dealt, w1_raw, 0)
+        deal_half(nc.vector.tensor_copy, w1_dealt, w1_raw, 1)
+        w1_q = quantize(dealt_planes(w1_dealt, 0, PLANES), "w1")
 
-        xq_words = keep.tile([P, S], U32, name="xq_words", align_bytes=64, tag="xq_words")
+        xq_words = keep.tile([P, S], U32, name="xq_words", align_bytes=ALIGN)
         for u in range(2):
             nc.vector.tensor_copy(xq_words[:, halves[u]], xw_all[:].bitcast(U32).indirect(half_of(offs_t, u)))
-        xq = (xq_words, xq_scales)
 
-        y = []
-        for t in range(PACK):
-            y_t = keep.tile([P, S], F32, name="y%d" % t)
+        y = per_plane("y", [P, S])
+        for t in range(PLANES):
             for u, cols in enumerate(halves if t == 0 else [slice(0, S)]):
-                acc = psum.tile([P, cols.stop - cols.start], F32, name="y_acc%d_%d" % (t, u), tag="bank%d" % (t + PACK * u))
-                mx_pass(acc[:], w1_q, t, xq, cols, True, True)
-                nc.scalar.copy(y_t[:, cols], acc[:])
-            y.append(y_t)
+                y_acc = bank(t + PLANES * u, cols.stop - cols.start, "y_acc%d_%d" % (t, u))
+                mx_pass(y_acc[:], w1_q, t, (xq_words, xq_scales), cols, True, True)
+                nc.scalar.copy(y[t][:, cols], y_acc[:])
 
-        w2_bf = keep.tile([P, PACK, P, PACK], BF16, name="w2_bf", align_bytes=64, tag="w1_codes")
-        w3_bf = keep.tile([P, PACK, P, PACK], BF16, name="w3_bf", align_bytes=64, tag="xq_words")
-        late_weights = [(w2_bf, w2_raw, 0), (w2_bf, w2_raw, 1), (w3_bf, w3_raw, 0), (w3_bf, w3_raw, 1)]
-        z_planes = keep.tile([P, PACK, S], BF16, name="z_planes", align_bytes=64, tag="z_planes")
-        h_window = [keep.tile([P, 2 * S], F32, name="h_window%d" % t, tag="h_window%d" % t) for t in range(PACK)]
-        h = [w[:, 0:S] for w in h_window]
-        sig = [w[:, S : 2 * S] for w in h_window]
-        pa_neg = [keep.tile([P, HALF], F32, name="pa_neg%d" % t) for t in range(PACK)]
-        pb = [keep.tile([P, HALF], F32, name="pb%d" % t) for t in range(PACK)]
-        st = [keep.tile([P, S], F32, name="st%d" % t) for t in range(PACK)]
-        st_copy = [keep.tile([P, S], F32, name="st_copy%d" % t) for t in range(PACK)]
-
-        ra = [keep.tile([P, HALF], F32, name="ra%d" % t, align_bytes=64, tag="ra%d" % t) for t in range(PACK)]
-        rb = [keep.tile([P, HALF], F32, name="rb%d" % t, align_bytes=64, tag="rb%d" % t) for t in range(PACK)]
-        dt = [keep.tile([P, S], F32, name="dt%d" % t, align_bytes=64, tag="dt%d" % t) for t in range(PACK)]
-        last = PACK - 1
-
-        for t in range(PACK):
-            nc.vector.tensor_scalar(pa_neg[t][:], y[t][:].indirect(n1_t[:]), -0.5, 0.0, ALU.mult, ALU.add)
-            nc.vector.tensor_copy(pb[t][:], y[t][:].indirect(n2_t[:]))
-            nc.gpsimd.tensor_tensor(pb[t][:], pb[t][:], pa_neg[t][:], ALU.add)
-            nc.gpsimd.tensor_tensor(ra[t][:], pb[t][:], pa_neg[t][:], ALU.add)
-        for t in range(PACK):
+        low, gap = per_plane("low", [P, HALF]), per_plane("gap", [P, HALF])
+        ra, rb = per_plane("ra", [P, HALF]), per_plane("rb", [P, HALF], ALIGN)
+        dt = per_plane("dt", [P, S], ALIGN)
+        for t in range(PLANES):
+            nc.vector.tensor_scalar(low[t][:], y[t][:].indirect(n1_t[:]), -0.5, 0.0, ALU.mult, ALU.add)
+            nc.vector.tensor_copy(gap[t][:], y[t][:].indirect(n2_t[:]))
+            nc.gpsimd.tensor_tensor(gap[t][:], gap[t][:], low[t][:], ALU.add)
+            nc.gpsimd.tensor_tensor(ra[t][:], gap[t][:], low[t][:], ALU.add)
+        for t in range(PLANES):
             nc.vector.tensor_copy(dt[t][:].indirect(n1_t[:]), ra[t][:])
 
-        for t in range(PACK):
+        h_wide = per_plane("h_wide", [P, 2 * S])
+        h = [tile[:, 0:S] for tile in h_wide]
+        sig = [tile[:, S : 2 * S] for tile in h_wide]
+        st, st_copy = per_plane("st", [P, S]), per_plane("st_copy", [P, S])
+        for t in range(PLANES):
             for u in range(2):
                 nc.scalar.activation(sig[t][:, halves[u]], y[t][:].indirect(half_of(n3_t, u)), ACT.Sigmoid)
-            nc.scalar.activation(rb[t][:], pb[t][:], ACT.Relu)
-            nc.gpsimd.tensor_tensor(rb[t][:], rb[t][:], pa_neg[t][:], ALU.subtract)
+            nc.scalar.activation(rb[t][:], gap[t][:], ACT.Relu)
+            nc.gpsimd.tensor_tensor(rb[t][:], rb[t][:], low[t][:], ALU.subtract)
             nc.scalar.activation(st[t][:], y[t][:], ACT.Copy, scale=gm_t[:, t : t + 1])
             nc.gpsimd.tensor_tensor(st[t][:], st[t][:], sig[t], ALU.mult)
             nc.sync.dma_start(st_copy[t][:], st[t][:])
-        for weights in late_weights:
-            deal_weight_half(nc.scalar.copy, *weights)
-        for t in range(PACK):
+
+        w2_dealt = keep.tile([P, PLANES, P, PLANES], BF16, name="w2_dealt", align_bytes=ALIGN)
+        w3_dealt = keep.tile([P, PLANES, P, PLANES], BF16, name="w3_dealt", align_bytes=ALIGN)
+        for dealt, raw in ((w2_dealt, w2_raw), (w3_dealt, w3_raw)):
+            for u in range(2):
+                deal_half(nc.scalar.copy, dealt, raw, u)
+
+        z_planes = [
+            keep.tile([P, PLANES, HALF], BF16, name="z_planes%d" % u, align_bytes=ALIGN, tag="z_planes%d" % u)
+            for u in range(2)
+        ]
+
+        def round_z(t, u):
+            nc.scalar.activation(z_planes[u][:, t, :], dt[t][:, halves[u]], ACT.Copy, scale=gn_t[:, t : t + 1])
+
+        for t in range(PLANES):
             nc.vector.tensor_copy(dt[t][:].indirect(n2_t[:]), rb[t][:])
-            nc.scalar.activation(z_planes[:, t, :], dt[t][:], ACT.Copy, scale=gn_t[:, t : t + 1])
+            if t < LAST:
+                for u in range(2):
+                    round_z(t, u)
+
+        w2_q = quantize(dealt_planes(w2_dealt, 0, PLANES), "w2", "rb%d" % (LAST - 1))
+        w3_first = quantize(dealt_planes(w3_dealt, 0, 1), "w3_first", "dt%d" % (LAST - 1))
+        z_grouped = []
+        for u in range(2):
+            round_z(LAST, u)
+            z_grouped.append(interleave(nc.scalar.copy, z_planes[u][:], "z_grouped%d" % u, "z_grouped%d" % u))
+
+        def fetch_z2(u, tag):
+            planes = keep.tile([P, PLANES, HALF], F32, name="z2_planes%d" % u, align_bytes=ALIGN, tag=tag)
+            for t in range(PLANES):
+                nc.vector.tensor_tensor(
+                    planes[:, t, :], st[t][:].indirect(half_of(n4_t, u)), st_copy[t][:, halves[u]], ALU.subtract
+                )
+            return planes[:]
 
         def negate_on_scalar(dst, src):
             nc.scalar.activation(dst, src, ACT.Copy, scale=-1.0)
@@ -172,130 +205,105 @@ def tile_picked_joinlifthopgkern_none_p_kernel(
         def negate_on_vector(dst, src):
             nc.vector.tensor_scalar(dst, src, -1.0, None, ALU.mult)
 
-        def quantize_tiles(w_bf, first, last, name, tag=""):
-            return quantize(w_bf[:, first:last].rearrange("p t m j -> p (t m j)"), name, tag)
-
-        w2_q = quantize_tiles(w2_bf, 0, PACK, "w2", "rb%d" % (last - 1))
-        w3_first = quantize_tiles(w3_bf, 0, 1, "w3_first", "dt%d" % (last - 1))
-        z_grouped = interleave(nc.scalar.copy, z_planes[:], "z_grouped", "z_grouped")
-
-        z2_planes = [
-            keep.tile([P, PACK, HALF], F32, name="z2_planes%d" % u, align_bytes=64, tag=("rb%d" % last, "z_grouped")[u])
-            for u in range(2)
-        ]
-
-        def fetch_z2(u, t):
-            nc.vector.tensor_tensor(
-                z2_planes[u][:, t, :], st[t][:].indirect(half_of(n4_t, u)), st_copy[t][:, halves[u]], ALU.subtract
-            )
-
-        for t in range(PACK):
-            fetch_z2(0, t)
-        z2_grouped0 = interleave(negate_on_scalar, z2_planes[0][:], "z2_grouped0", "z_planes")
-        z_q = quantize(z_grouped, "z")
-        for t in range(PACK):
-            fetch_z2(1, t)
+        z2_grouped0 = interleave(negate_on_scalar, fetch_z2(0, "rb%d" % LAST), "z2_grouped0", "z_planes1")
+        z_q = [quantize(z_grouped[u], "z%d" % u) for u in range(2)]
+        z2_planes1 = fetch_z2(1, "z_grouped0")
         z2_q0 = quantize(z2_grouped0, "z2a")
-        z2_grouped1 = interleave(negate_on_vector, z2_planes[1][:], "z2_grouped1", "z_planes")
+        z2_grouped1 = interleave(negate_on_vector, z2_planes1, "z2_grouped1", "z_planes1")
         z2_q = [z2_q0, quantize(z2_grouped1, "z2b")]
 
         warm_exp = keep.tile([P, 1], F32, name="warm_exp")
         nc.scalar.activation(warm_exp[:], z2_grouped0[:, 0:1], ACT.Exp, scale=0.0)
-        acc = [
-            [psum.tile([P, HALF], F32, name="h_acc%d_%d" % (t, u), tag="bank%d" % (t + PACK * u)) for u in range(2)]
-            for t in range(PACK)
-        ]
-        for t in range(PACK):
+        h_acc = [[bank(t + PLANES * u, HALF, "h_acc%d_%d" % (t, u)) for u in range(2)] for t in range(PLANES)]
+        for t in range(PLANES):
             for u in range(2):
-                mx_pass(acc[t][u][:], w2_q, t, z_q, halves[u], True, False)
+                mx_pass(h_acc[t][u][:], w2_q, t, z_q[u], halves[0], True, False)
 
-        def close(t, weights, column_block):
+        def close(t, weights, block):
             for u in range(2):
-                mx_pass(acc[t][u][:], weights, column_block, z2_q[u], slice(0, HALF), False, True)
-                nc.scalar.copy(h[t][:, halves[u]], acc[t][u][:])
+                mx_pass(h_acc[t][u][:], weights, block, z2_q[u], halves[0], False, True)
+                nc.scalar.copy(h[t][:, halves[u]], h_acc[t][u][:])
 
         close(0, w3_first, 0)
-        late = keep.tile([P, 3 * P], U32, name="late_codes", align_bytes=64, tag="z_grouped")
-        late_scales = keep.tile([P, 3 * P], U8, name="late_scales", align_bytes=64)
-        for first, stop in ((1, 2), (2, 4)):
+        w3_late = (
+            keep.tile([P, LAST * P], U32, name="w3_late_codes", align_bytes=ALIGN, tag="z_grouped0"),
+            keep.tile([P, LAST * P], U8, name="w3_late_scales", align_bytes=ALIGN),
+        )
+        for first, stop in ((1, 2), (2, PLANES)):
             cols = slice((first - 1) * P, (stop - 1) * P)
             nc.vector.quantize_mx(
-                out=late[:, cols].bitcast(FP8X4),
-                scales=late_scales[:, cols],
-                in_=w3_bf[:, first:stop].rearrange("p t m j -> p (t m j)"),
+                out=w3_late[0][:, cols].bitcast(FP8X4),
+                scales=w3_late[1][:, cols],
+                in_=dealt_planes(w3_dealt, first, stop),
             )
-        for t in range(1, PACK):
-            close(t, (late, late_scales), t - 1)
+        for t in range(1, PLANES):
+            close(t, w3_late, t - 1)
 
-        blocks = [slice(b * P, (b + 1) * P) for b in range(S // P)]
-        picked = [keep.tile([P, 2, S], F32, name="picked%d" % t, tag="picked%d" % t) for t in range(PACK)]
-        weight = [keep.tile([P, 2, S], F32, name="weight%d" % t) for t in range(PACK)]
-        diff = [keep.tile([P, 2, S], F32, name="diff%d" % t) for t in range(PACK)]
-        den_sq = [keep.tile([P, S], F32, name="den_sq%d" % t) for t in range(PACK)]
+        picked, kr, diff = per_plane("picked", [P, 2, S]), per_plane("kr", [P, 2, S]), per_plane("diff", [P, 2, S])
+        den_sq, prod, num = [], [], []
 
-        def fetch(t, a):
-            nc.vector.tensor_copy(picked[t][:, a, :], h_window[t][:].indirect((n5_t, n6_t)[a][:]))
+        def fetch(t, side):
+            nc.vector.tensor_copy(picked[t][:, side, :], h_wide[t][:].indirect((n5_t, n6_t)[side][:]))
 
-        def weigh(t, a):
-            nc.scalar.activation(diff[t][:, a, :], diff[t][:, a, :], ACT.Square)
-            nc.scalar.activation(weight[t][:, a, :], diff[t][:, a, :], ACT.Exp, scale=-0.5)
+        def weigh(t, side):
+            nc.scalar.activation(diff[t][:, side, :], diff[t][:, side, :], ACT.Square)
+            nc.scalar.activation(kr[t][:, side, :], diff[t][:, side, :], ACT.Exp, scale=-0.5)
 
-        def denominator(t):
-            sum_t = psum.tile([P, S], F32, name="sum%d" % t, tag="bank%d" % (PACK + t))
+        def denominator(t, turned):
+            total = bank(PLANES + t, S, "total%d" % t)
             for b in blocks:
-                for a in range(2):
+                for side in range(2):
                     nc.tensor.matmul(
-                        sum_t[:, b], weight[t][:, a, b], ident[:], start=(a == 0), stop=(a == 1), is_transpose=True
+                        total[:, b], kr[t][:, side, b], ident[:], start=(side == 0), stop=(side == 1), is_transpose=True
                     )
-            nc.scalar.activation(den_sq[t][:], sum_t[:], ACT.Square, bias=0.5)
-
-        prod, num = [], []
+            nc.scalar.activation(turned, total[:], ACT.Square, bias=0.5)
+            back = bank(t, S, "den_sq%d" % t)
+            for b in blocks:
+                nc.tensor.transpose(back[:, b], turned[:, b], ident[:])
+            den_sq.append(back)
 
         def products(t):
-            prod_t = keep.tile([P, 2, S], F32, name="prod%d" % t, tag="h_window%d" % ((t + 2) % PACK))
-            nc.vector.tensor_tensor(prod_t[:], picked[t][:], weight[t][:], ALU.mult)
-            prod.append(prod_t)
+            tile = keep.tile([P, 2, S], F32, name="prod%d" % t, tag="h_wide%d" % ((t + 2) % PLANES))
+            nc.vector.tensor_tensor(tile[:], picked[t][:], kr[t][:], ALU.mult)
+            prod.append(tile)
 
         def numerator(t):
-            num_t = keep.tile([P, S], F32, name="num%d" % t, tag="picked%d" % ((t + 1) % PACK))
-            nc.vector.tensor_tensor(num_t[:], prod[t][:, 0, :], prod[t][:, 1, :], ALU.add)
-            num.append(num_t)
+            tile = keep.tile([P, S], F32, name="num%d" % t)
+            nc.vector.tensor_tensor(tile[:], prod[t][:, 0, :], prod[t][:, 1, :], ALU.add)
+            num.append(tile)
 
-        out_rows = out.rearrange("(p t) j -> p t j", t=PACK)
+        out_planes = out.rearrange("(p t) j -> p t j", t=PLANES)
 
-        def finish(t, cols, bank):
-            width = cols.stop - cols.start
-            inv = keep.tile([P, width], F32, name="inv%d" % bank)
-            nc.scalar.activation(inv[:], den_sq[t][:, cols], ACT.Abs_reciprocal_sqrt)
-            inv_back = psum.tile([P, width], F32, name="inv_back%d" % bank, tag="bank%d" % bank)
-            for b in blocks[: width // P]:
-                nc.tensor.transpose(inv_back[:, b], inv[:, b], ident[:])
-            nc.vector.tensor_tensor(num[t][:, cols], num[t][:, cols], inv_back[:], ALU.mult)
-            nc.sync.dma_start(out_rows[:, t, cols], num[t][:, cols])
+        def finish(t, pieces):
+            nc.scalar.activation(inv[:, t, :], den_sq[t][:], ACT.Abs_reciprocal_sqrt)
+            for cols in pieces:
+                nc.vector.tensor_tensor(num[t][:, cols], num[t][:, cols], inv[:, t, cols], ALU.mult)
+                nc.sync.dma_start(out_planes[:, t, cols], num[t][:, cols])
 
-        for t in range(last):
-            for a in range(2):
-                fetch(t, a)
-                nc.gpsimd.tensor_tensor(diff[t][:, a, :], picked[t][:, a, :], h[t], ALU.subtract)
-                weigh(t, a)
-                if a == 0 and t > 0:
-                    denominator(t - 1)
-        for a in range(2):
-            fetch(last, a)
+        for t in range(LAST):
+            for side in range(2):
+                fetch(t, side)
+                nc.gpsimd.tensor_tensor(diff[t][:, side, :], picked[t][:, side, :], h[t], ALU.subtract)
+                weigh(t, side)
+            if t > 0:
+                denominator(t - 1, keep.tile([P, S], F32, name="turned%d" % (t - 1))[:])
+        for side in range(2):
+            fetch(LAST, side)
         nc.vector.tensor_tensor(
-            diff[last][:], picked[last][:], h[last].unsqueeze(1).to_broadcast([P, 2, S]), ALU.subtract
+            diff[LAST][:], picked[LAST][:], h[LAST].unsqueeze(1).to_broadcast([P, 2, S]), ALU.subtract
         )
-        weigh(last, 0)
-        denominator(last - 1)
-        weigh(last, 1)
-        denominator(last)
+        for side in range(2):
+            weigh(LAST, side)
+        inv = keep.tile([P, PLANES, S], F32, name="inv", tag="diff%d" % LAST)
+        denominator(LAST - 1, keep.tile([P, S], F32, name="turned%d" % (LAST - 1))[:])
+        denominator(LAST, inv[:, LAST, :])
+
         products(0)
-        for t in range(1, PACK):
+        for t in range(1, PLANES):
             products(t)
             numerator(t - 1)
-        finish(0, slice(0, S), 0)
-        numerator(last)
-        for t in range(1, last):
-            finish(t, slice(0, S), t)
-        for u in range(2):
-            finish(last, halves[u], last + u)
+        finish(0, [slice(0, S)])
+        numerator(LAST)
+        for t in range(1, LAST):
+            finish(t, [slice(0, S)])
+        finish(LAST, halves)

from contextlib import ExitStack

import concourse.mybir as mybir
from concourse.masks import make_identity

F32 = mybir.dt.float32
BF16 = mybir.dt.bfloat16
I32 = mybir.dt.int32
U32 = mybir.dt.uint32
U16 = mybir.dt.uint16
U8 = mybir.dt.uint8
FP8X4 = mybir.dt.float8_e4m3fn_x4
ALU = mybir.AluOpType
ACT = mybir.ActivationFunctionType

P = 128
PLANES = 4
LAST = PLANES - 1
T = 2048
S = 512
HALF = S // 2
LIST_ROWS = 16
LINE = 4
ALIGN = 64
FLOPS = 3 * 2 * 512 * 512 * 512


def tile_picked_joinlifthopgkern_none_p_kernel(
    tc, x_words, x_scales, w1, gn, gm, w2, w3, offs, n1, n2, n3, n4, n5, n6, out
):
    nc = tc.nc
    halves = [slice(0, HALF), slice(HALF, S)]
    blocks = [slice(b * P, (b + 1) * P) for b in range(S // P)]

    with ExitStack() as ctx:
        lists = ctx.enter_context(tc.tile_pool(name="lists", bufs=1))
        keep = ctx.enter_context(tc.tile_pool(name="keep", bufs=1))
        psum = ctx.enter_context(tc.psum_pool(name="psum", bufs=1))

        def per_plane(name, shape, align=None):
            return [
                keep.tile(shape, F32, name="%s%d" % (name, t), tag="%s%d" % (name, t), align_bytes=align)
                for t in range(PLANES)
            ]

        def bank(number, width, name):
            return psum.tile([P, width], F32, name=name, tag="bank%d" % number)

        def load_list(source, name):
            tile = lists.tile([P, source.shape[1]], U16, name=name)
            nc.sync.dma_start(tile[:], source)
            return tile

        def half_of(list_tile, u):
            columns = HALF // LIST_ROWS
            return list_tile[:, u * columns : (u + 1) * columns]

        def load_weight(w, name):
            raw = keep.tile([P, PLANES, S], F32, name=name)
            nc.sync.dma_start(raw[:], w.rearrange("(p j) c -> p j c", j=PLANES))
            return raw

        def load_gain(gain, name):
            tile = keep.tile([P, PLANES], F32, name=name)
            nc.sync.dma_start(tile[:], gain.rearrange("(p t) o -> p (t o)", t=PLANES))
            return tile

        def deal_half(copy, dealt, raw, u):
            m_half = slice(u * P // 2, (u + 1) * P // 2)
            copy(
                dealt[:, :, m_half, :].rearrange("p t m j -> p m j t"),
                raw[:, :, halves[u]].rearrange("p j (m t) -> p m j t", t=PLANES),
            )

        def interleave(copy, planes, name, tag):
            grouped = keep.tile([P, planes.shape[2], PLANES], BF16, name=name, align_bytes=ALIGN, tag=tag)
            copy(
                grouped[:].rearrange("p (c i) t -> p c t i", i=LINE),
                planes.rearrange("p t (c i) -> p c t i", i=LINE),
            )
            return grouped[:].rearrange("p c t -> p (c t)")

        def quantize(grouped, name, tag=""):
            width = grouped.shape[1] // PLANES
            codes = keep.tile([P, width], U32, name=name + "_codes", align_bytes=ALIGN, tag=tag)
            scales = keep.tile([P, width], U8, name=name + "_scales", align_bytes=ALIGN)
            nc.vector.quantize_mx(out=codes[:].bitcast(FP8X4), scales=scales[:], in_=grouped)
            return codes, scales

        def dealt_planes(dealt, first, stop):
            return dealt[:, first:stop].rearrange("p t m j -> p (t m j)")

        def mx_pass(acc, weights, block, moving, cols, start, stop):
            nc.tensor.matmul_mx(
                out=acc,
                lhsT=weights[0][:, blocks[block]].bitcast(FP8X4),
                lhsT_scale=weights[1][:, blocks[block]],
                rhs=moving[0][:, cols].bitcast(FP8X4),
                rhs_scale=moving[1][:, cols],
                start=start,
                stop=stop,
            )

        xs_all = keep.tile([P, T], U8, name="xs_all")
        nc.gpsimd.memset(xs_all[:].bitcast(I32), 0)
        for q in range(4):
            nc.scalar.dma_start(
                xs_all[32 * q : 32 * q + 4, :].bitcast(I32), x_scales[0, 4 * q : 4 * q + 4, :].bitcast(I32)
            )
        warm = keep.tile([P, 2], F32, name="warm")
        nc.gpsimd.memset(warm[:, 0:1], 0.0)
        nc.scalar.activation(warm[:, 1:2], warm[:, 0:1], ACT.Sigmoid)
        offs_t = load_list(offs, "offs")
        w1_raw = load_weight(w1, "w1_raw")
        xw_all = keep.tile([P, T], I32, name="xw_all")
        nc.sync.dma_start(xw_all[:], x_words[0].rearrange("p n t -> p (n t)").bitcast(I32))
        n1_t, n2_t, n3_t = load_list(n1, "n1"), load_list(n2, "n2"), load_list(n3, "n3")
        gn_t, gm_t = load_gain(gn, "gn_t"), load_gain(gm, "gm_t")
        w2_raw, w3_raw = load_weight(w2, "w2_raw"), load_weight(w3, "w3_raw")
        n4_t, n5_t, n6_t = load_list(n4, "n4"), load_list(n5, "n5"), load_list(n6, "n6")

        ident = keep.tile([P, P], F32, name="ident")
        make_identity(nc, ident[:])

        xq_scales = keep.tile([P, S], U8, name="xq_scales", align_bytes=ALIGN)
        nc.vector.tensor_copy(xq_scales[:], xs_all[:].indirect(offs_t[:]))
        w1_dealt = keep.tile([P, PLANES, P, PLANES], BF16, name="w1_dealt", align_bytes=ALIGN)
        deal_half(nc.scalar.copy, w1_dealt, w1_raw, 0)
        deal_half(nc.vector.tensor_copy, w1_dealt, w1_raw, 1)
        w1_q = quantize(dealt_planes(w1_dealt, 0, PLANES), "w1")

        xq_words = keep.tile([P, S], U32, name="xq_words", align_bytes=ALIGN)
        for u in range(2):
            nc.vector.tensor_copy(xq_words[:, halves[u]], xw_all[:].bitcast(U32).indirect(half_of(offs_t, u)))

        y = per_plane("y", [P, S])
        for t in range(PLANES):
            for u, cols in enumerate(halves if t == 0 else [slice(0, S)]):
                y_acc = bank(t + PLANES * u, cols.stop - cols.start, "y_acc%d_%d" % (t, u))
                mx_pass(y_acc[:], w1_q, t, (xq_words, xq_scales), cols, True, True)
                nc.scalar.copy(y[t][:, cols], y_acc[:])

        low, gap = per_plane("low", [P, HALF]), per_plane("gap", [P, HALF])
        ra, rb = per_plane("ra", [P, HALF]), per_plane("rb", [P, HALF], ALIGN)
        dt = per_plane("dt", [P, S], ALIGN)
        for t in range(PLANES):
            nc.vector.tensor_scalar(low[t][:], y[t][:].indirect(n1_t[:]), -0.5, 0.0, ALU.mult, ALU.add)
            nc.vector.tensor_copy(gap[t][:], y[t][:].indirect(n2_t[:]))
            nc.gpsimd.tensor_tensor(gap[t][:], gap[t][:], low[t][:], ALU.add)
            nc.gpsimd.tensor_tensor(ra[t][:], gap[t][:], low[t][:], ALU.add)
        for t in range(PLANES):
            nc.vector.tensor_copy(dt[t][:].indirect(n1_t[:]), ra[t][:])

        h_wide = per_plane("h_wide", [P, 2 * S])
        h = [tile[:, 0:S] for tile in h_wide]
        sig = [tile[:, S : 2 * S] for tile in h_wide]
        st, st_copy = per_plane("st", [P, S]), per_plane("st_copy", [P, S])
        for t in range(PLANES):
            for u in range(2):
                nc.scalar.activation(sig[t][:, halves[u]], y[t][:].indirect(half_of(n3_t, u)), ACT.Sigmoid)
            nc.scalar.activation(rb[t][:], gap[t][:], ACT.Relu)
            nc.gpsimd.tensor_tensor(rb[t][:], rb[t][:], low[t][:], ALU.subtract)
            nc.scalar.activation(st[t][:], y[t][:], ACT.Copy, scale=gm_t[:, t : t + 1])
            nc.gpsimd.tensor_tensor(st[t][:], st[t][:], sig[t], ALU.mult)
            nc.sync.dma_start(st_copy[t][:], st[t][:])

        w2_dealt = keep.tile([P, PLANES, P, PLANES], BF16, name="w2_dealt", align_bytes=ALIGN)
        w3_dealt = keep.tile([P, PLANES, P, PLANES], BF16, name="w3_dealt", align_bytes=ALIGN)
        for dealt, raw in ((w2_dealt, w2_raw), (w3_dealt, w3_raw)):
            for u in range(2):
                deal_half(nc.scalar.copy, dealt, raw, u)

        z_planes = [
            keep.tile([P, PLANES, HALF], BF16, name="z_planes%d" % u, align_bytes=ALIGN, tag="z_planes%d" % u)
            for u in range(2)
        ]

        def round_z(t, u):
            nc.scalar.activation(z_planes[u][:, t, :], dt[t][:, halves[u]], ACT.Copy, scale=gn_t[:, t : t + 1])

        for t in range(PLANES):
            nc.vector.tensor_copy(dt[t][:].indirect(n2_t[:]), rb[t][:])
            if t < LAST:
                for u in range(2):
                    round_z(t, u)

        w2_q = quantize(dealt_planes(w2_dealt, 0, PLANES), "w2", "rb%d" % (LAST - 1))
        w3_first = quantize(dealt_planes(w3_dealt, 0, 1), "w3_first", "dt%d" % (LAST - 1))
        z_grouped = []
        for u in range(2):
            round_z(LAST, u)
            z_grouped.append(interleave(nc.scalar.copy, z_planes[u][:], "z_grouped%d" % u, "z_grouped%d" % u))

        def fetch_z2(u, tag):
            planes = keep.tile([P, PLANES, HALF], F32, name="z2_planes%d" % u, align_bytes=ALIGN, tag=tag)
            for t in range(PLANES):
                nc.vector.tensor_tensor(
                    planes[:, t, :], st[t][:].indirect(half_of(n4_t, u)), st_copy[t][:, halves[u]], ALU.subtract
                )
            return planes[:]

        def negate_on_scalar(dst, src):
            nc.scalar.activation(dst, src, ACT.Copy, scale=-1.0)

        def negate_on_vector(dst, src):
            nc.vector.tensor_scalar(dst, src, -1.0, None, ALU.mult)

        z2_grouped0 = interleave(negate_on_scalar, fetch_z2(0, "rb%d" % LAST), "z2_grouped0", "z_planes1")
        z_q = [quantize(z_grouped[u], "z%d" % u) for u in range(2)]
        z2_planes1 = fetch_z2(1, "z_grouped0")
        z2_q0 = quantize(z2_grouped0, "z2a")
        z2_grouped1 = interleave(negate_on_vector, z2_planes1, "z2_grouped1", "z_planes1")
        z2_q = [z2_q0, quantize(z2_grouped1, "z2b")]

        warm_exp = keep.tile([P, 1], F32, name="warm_exp")
        nc.scalar.activation(warm_exp[:], z2_grouped0[:, 0:1], ACT.Exp, scale=0.0)
        h_acc = [[bank(t + PLANES * u, HALF, "h_acc%d_%d" % (t, u)) for u in range(2)] for t in range(PLANES)]
        for t in range(PLANES):
            for u in range(2):
                mx_pass(h_acc[t][u][:], w2_q, t, z_q[u], halves[0], True, False)

        def close(t, weights, block):
            for u in range(2):
                mx_pass(h_acc[t][u][:], weights, block, z2_q[u], halves[0], False, True)
                nc.scalar.copy(h[t][:, halves[u]], h_acc[t][u][:])

        close(0, w3_first, 0)
        w3_late = (
            keep.tile([P, LAST * P], U32, name="w3_late_codes", align_bytes=ALIGN, tag="z_grouped0"),
            keep.tile([P, LAST * P], U8, name="w3_late_scales", align_bytes=ALIGN),
        )
        for first, stop in ((1, 2), (2, PLANES)):
            cols = slice((first - 1) * P, (stop - 1) * P)
            nc.vector.quantize_mx(
                out=w3_late[0][:, cols].bitcast(FP8X4),
                scales=w3_late[1][:, cols],
                in_=dealt_planes(w3_dealt, first, stop),
            )
        for t in range(1, PLANES):
            close(t, w3_late, t - 1)

        picked, kr, diff = per_plane("picked", [P, 2, S]), per_plane("kr", [P, 2, S]), per_plane("diff", [P, 2, S])
        den_sq, prod, num = [], [], []

        def fetch(t, side):
            nc.vector.tensor_copy(picked[t][:, side, :], h_wide[t][:].indirect((n5_t, n6_t)[side][:]))

        def weigh(t, side):
            nc.scalar.activation(diff[t][:, side, :], diff[t][:, side, :], ACT.Square)
            nc.scalar.activation(kr[t][:, side, :], diff[t][:, side, :], ACT.Exp, scale=-0.5)

        def denominator(t, turned):
            total = bank(PLANES + t, S, "total%d" % t)
            for b in blocks:
                for side in range(2):
                    nc.tensor.matmul(
                        total[:, b], kr[t][:, side, b], ident[:], start=(side == 0), stop=(side == 1), is_transpose=True
                    )
            nc.scalar.activation(turned, total[:], ACT.Square, bias=0.5)
            back = bank(t, S, "den_sq%d" % t)
            for b in blocks:
                nc.tensor.transpose(back[:, b], turned[:, b], ident[:])
            den_sq.append(back)

        def products(t):
            tile = keep.tile([P, 2, S], F32, name="prod%d" % t, tag="h_wide%d" % ((t + 2) % PLANES))
            nc.vector.tensor_tensor(tile[:], picked[t][:], kr[t][:], ALU.mult)
            prod.append(tile)

        def numerator(t):
            tile = keep.tile([P, S], F32, name="num%d" % t)
            nc.vector.tensor_tensor(tile[:], prod[t][:, 0, :], prod[t][:, 1, :], ALU.add)
            num.append(tile)

        out_planes = out.rearrange("(p t) j -> p t j", t=PLANES)

        def finish(t, pieces):
            nc.scalar.activation(inv[:, t, :], den_sq[t][:], ACT.Abs_reciprocal_sqrt)
            for cols in pieces:
                nc.vector.tensor_tensor(num[t][:, cols], num[t][:, cols], inv[:, t, cols], ALU.mult)
                nc.sync.dma_start(out_planes[:, t, cols], num[t][:, cols])

        for t in range(LAST):
            for side in range(2):
                fetch(t, side)
                nc.gpsimd.tensor_tensor(diff[t][:, side, :], picked[t][:, side, :], h[t], ALU.subtract)
                weigh(t, side)
            if t > 0:
                denominator(t - 1, keep.tile([P, S], F32, name="turned%d" % (t - 1))[:])
        for side in range(2):
            fetch(LAST, side)
        nc.vector.tensor_tensor(
            diff[LAST][:], picked[LAST][:], h[LAST].unsqueeze(1).to_broadcast([P, 2, S]), ALU.subtract
        )
        for side in range(2):
            weigh(LAST, side)
        inv = keep.tile([P, PLANES, S], F32, name="inv", tag="diff%d" % LAST)
        denominator(LAST - 1, keep.tile([P, S], F32, name="turned%d" % (LAST - 1))[:])
        denominator(LAST, inv[:, LAST, :])

        products(0)
        for t in range(1, PLANES):
            products(t)
            numerator(t - 1)
        finish(0, [slice(0, S)])
        numerator(LAST)
        for t in range(1, LAST):
            finish(t, [slice(0, S)])
        finish(LAST, halves)
